import numpy as np
import ml_dtypes


def mxq(x, axis, fmt="e4m3"):
    dtype, down = {"e4m3": (ml_dtypes.float8_e4m3fn, 7), "e5m2": (ml_dtypes.float8_e5m2, 14)}[fmt]
    v = np.moveaxis(np.asarray(x, np.float32).astype(ml_dtypes.bfloat16).astype(np.float64), axis, -1)
    blocks = v.reshape(v.shape[:-1] + (-1, 32))
    amax = np.abs(blocks).max(-1, keepdims=True)
    byte = np.maximum(np.where(amax > 0, np.frexp(amax)[1] - 1 + 127, 0) - down, 1)
    scale = np.exp2(byte - 127.0)
    codes = (blocks / scale).astype(np.float32).astype(dtype).astype(np.float64)
    return np.moveaxis((codes * scale).reshape(v.shape), -1, axis)


WIDE = False


def mx_kscale(k):
    if not WIDE:
        return np.ones(k)
    levels = np.array([10, -10, 5, -5, 0])
    if k % 512:
        return np.exp2(np.random.permutation(np.resize(levels, k // 32))).repeat(32)
    a = np.empty((k // 512, 16))
    for p in range(k // 512):
        a[p, :8] = np.random.permutation(np.resize(levels, 8))
        for g in range(8):
            far = levels[np.abs(levels - a[p, g]) >= 10]
            a[p, g + 8] = far[np.random.randint(len(far))]
    return np.exp2(a.ravel()).repeat(32)


def f64(x):
    return np.asarray(x).astype(np.float64)


def striped(idx):
    return np.tile(idx.reshape(-1, 16).T, (8, 1)).astype(np.uint16)


def unstriped(offs):
    return offs[:16].T.reshape(-1).astype(np.int64)


def striped8(idx):
    return np.concatenate([x.reshape(-1, 16).T for x in idx]).astype(np.uint16)


def runs(offs, k):
    lists = np.stack([offs[16 * r : 16 * r + 16].T.reshape(-1) for r in range(8)]).astype(np.int64)
    return lists[np.arange(k) % 512 // 64]


def pack_weight(w):
    k, n = w.shape
    w = f64(np.asarray(w, np.float32).astype(ml_dtypes.bfloat16)).reshape(k // 32, 32, n)
    amax = np.abs(w).max(1)
    byte = np.clip(np.where(amax > 0, np.frexp(amax)[1] - 1 + 127 - 7, 1), 1, 254)
    scaled = (w * np.exp2(127.0 - byte)[:, None, :]).reshape(k, n).astype(np.float32)
    words = np.ascontiguousarray(scaled.reshape(k // 512, 128, 4, n).transpose(0, 1, 3, 2)).astype(ml_dtypes.float8_e4m3fn).view(np.uint8)
    return words, np.ascontiguousarray(byte.astype(np.uint8).reshape(k // 512, 16, n))


def unpack_weight(words, scales):
    g, p, n, _ = words.shape
    vals = np.ascontiguousarray(words).view(ml_dtypes.float8_e4m3fn).astype(np.float64) * np.repeat(np.exp2(scales.astype(np.float64) - 127.0), 8, axis=1)[..., None]
    return vals.transpose(0, 1, 3, 2).reshape(g * 512, n)


K, T, S, G, H, W, U = 512, 1024, 512, 2048, 512, 256, 1024


def setup_inputs():
    n = np.random.standard_normal
    s = mx_kscale(K)[:, None]
    packed_xT = pack_weight(n((K, T)) * s)
    packed_dT = pack_weight(n((K, G)) / s)
    perm = np.stack([np.random.permutation(S) for _ in range(8)])
    perm2 = np.stack([np.random.permutation(U) for _ in range(8)])
    return {
        "x_words": packed_xT[0],
        "x_scales": packed_xT[1],
        "d_words": packed_dT[0],
        "d_scales": packed_dT[1],
        "gs": (np.random.uniform(0.5, 1.5, (K, 1)) * s).astype(np.float32),
        "offs": striped(np.random.permutation(T)[:S]),
        "k1": striped8(np.random.randint(0, G, (8, H))),
        "hz": striped8(np.random.randint(0, T, (8, S))),
        "k2": striped8(np.random.randint(0, G, (8, H))),
        "hy": striped8(np.random.randint(0, T, (8, S))),
        "k3": striped8(np.random.randint(0, G, (8, H))),
        "n1": striped8(perm[:, :W]),
        "n2": striped8(perm[:, W:]),
        "n3": striped8(np.stack([np.random.permutation(S) for _ in range(8)])),
        "k4": striped8(np.random.randint(0, G, (8, H))),
        "k5": striped8(np.random.randint(0, G, (8, H))),
        "hx": striped8(np.random.randint(0, T, (8, S))),
        "n4": striped8(perm2[:, :S]),
        "n5": striped8(perm2[:, S:]),
        "n6": striped8(np.stack([np.random.permutation(S) for _ in range(8)])),
    }


def reference(x_words, x_scales, d_words, d_scales, gs, offs, k1, hz, k2, hy, k3, n1, n2, n3, k4, k5, hx, n4, n5, n6):
    d_k4 = unpack_weight(d_words, d_scales)[np.arange(K)[:, None], runs(k4, K)]
    d_k1 = unpack_weight(d_words, d_scales)[np.arange(K)[:, None], runs(k1, K)]
    xq = unpack_weight(x_words, x_scales)[:, unstriped(offs)]
    d_k2 = unpack_weight(d_words, d_scales)[np.arange(K)[:, None], runs(k2, K)]
    x_hz = unpack_weight(x_words, x_scales)[np.arange(K)[:, None], runs(hz, K)]
    d_k3 = unpack_weight(d_words, d_scales)[np.arange(K)[:, None], runs(k3, K)]
    x_hy = unpack_weight(x_words, x_scales)[np.arange(K)[:, None], runs(hy, K)]
    h = 0.0625 * (d_k1.T @ xq + d_k2.T @ x_hz + d_k3.T @ x_hy)
    pa = h[np.arange(H)[:, None], runs(n1, H)]
    pb = h[np.arange(H)[:, None], runs(n2, H)]
    rb = np.minimum(pa, pb)
    ra = np.maximum(pa, pb)
    ua = np.zeros((H, S))
    ua[np.arange(H)[:, None], runs(n1, H)] = ra
    ub = ua.copy()
    ub[np.arange(H)[:, None], runs(n2, H)] = rb
    z = f64(gs) * (ub - (ub[np.arange(H)[:, None], runs(n3, H)]))
    d_k5 = unpack_weight(d_words, d_scales)[np.arange(K)[:, None], runs(k5, K)]
    x_hx = unpack_weight(x_words, x_scales)[np.arange(K)[:, None], runs(hx, K)]
    h2 = 0.0625 * ((d_k4.T @ mxq(z, 0, "e4m3") + d_k5.T @ x_hx))
    ds = np.zeros((H, S))
    ds[np.arange(H)[:, None], runs(n6, H)] = h2
    up = np.maximum(h2, ds)
    ph = np.zeros((H, U))
    ph[np.arange(H)[:, None], runs(n4, H)] = ds
    out = ph.copy()
    out[np.arange(H)[:, None], runs(n5, H)] = up
    return out

@@ -1,0 +1,233 @@
+from contextlib import ExitStack
+
+import concourse.mybir as mybir
+from concourse.masks import make_identity
+
+F32 = mybir.dt.float32
+BF16 = mybir.dt.bfloat16
+I32 = mybir.dt.int32
+U32 = mybir.dt.uint32
+U16 = mybir.dt.uint16
+U8 = mybir.dt.uint8
+FP8X4 = mybir.dt.float8_e4m3fn_x4
+ALU = mybir.AluOpType
+COPY = mybir.ActivationFunctionType.Copy
+
+P = 128
+PACK = 4
+S = 512
+W = 256
+T = 1024
+G = 2048
+U = 1024
+BLOCK = 128
+NBLK = S // BLOCK
+FLOPS = 5 * 2 * 512 * 512 * 512
+
+
+def cols(first, count):
+    return slice(first, first + count)
+
+
+def entries(first, count):
+    return slice(first // 16, (first + count) // 16)
+
+
+def tile_picked_mthhzmhorddpagsn_none_p_kernel(
+    tc, x_words, x_scales, d_words, d_scales, gs, offs, k1, hz, k2, hy, k3, n1, n2, n3, k4, k5, hx, n4, n5, n6, out
+):
+    nc = tc.nc
+    with ExitStack() as ctx:
+        lists = ctx.enter_context(tc.tile_pool(name="lists", bufs=1))
+        keep = ctx.enter_context(tc.tile_pool(name="keep", bufs=1))
+        psum = ctx.enter_context(tc.psum_pool(name="psum", bufs=1))
+
+        def load_list(name, src):
+            tile = lists.tile([P, src.shape[1]], U16, name=name)
+            nc.sync.dma_start(tile[:], src)
+            return tile
+
+        d_rows = keep.tile([P, G], U8, name="d_rows", align_bytes=64)
+        x_rows = keep.tile([P, T], U8, name="x_rows", align_bytes=64)
+        plane_h = keep.tile([P, 6 * S], U8, name="plane_h", align_bytes=64)
+        plane_h2 = keep.tile([P, 3 * S], U8, name="plane_h2", align_bytes=64)
+        for tile in (d_rows, x_rows, plane_h, plane_h2):
+            nc.vector.memset(tile[:].bitcast(I32), 0)
+        nc.sync.dma_start(d_rows[0:P:8, :].bitcast(I32), d_scales[0].bitcast(I32))
+        l_k1 = load_list("l_k1", k1)
+        l_k2 = load_list("l_k2", k2)
+        l_k3 = load_list("l_k3", k3)
+        nc.sync.dma_start(x_rows[0:P:8, :].bitcast(I32), x_scales[0].bitcast(I32))
+        l_offs = load_list("l_offs", offs)
+        l_hz = load_list("l_hz", hz)
+        l_hy = load_list("l_hy", hy)
+        d_table = keep.tile([P, G], U32, name="d_table", align_bytes=64)
+        x_table = keep.tile([P, T], U32, name="x_table", align_bytes=64)
+        nc.sync.dma_start(d_table[:].bitcast(I32), d_words[0].rearrange("p n t -> p (n t)").bitcast(I32))
+        nc.sync.dma_start(x_table[:].bitcast(I32), x_words[0].rearrange("p n t -> p (n t)").bitcast(I32))
+        gs_sb = keep.tile([P, PACK], F32, name="gs_sb")
+        nc.sync.dma_start(gs_sb[:], gs.rearrange("(p t) o -> p (t o)", t=PACK))
+        l_k4 = load_list("l_k4", k4)
+        l_k5 = load_list("l_k5", k5)
+        l_hx = load_list("l_hx", hx)
+        l_n1 = load_list("l_n1", n1)
+        l_n2 = load_list("l_n2", n2)
+        l_n3 = load_list("l_n3", n3)
+        l_n6 = load_list("l_n6", n6)
+        l_n4 = load_list("l_n4", n4)
+        l_n5 = load_list("l_n5", n5)
+
+        ident = keep.tile([P, P], F32, name="ident")
+        make_identity(nc, ident[:])
+        gain = keep.tile([P, PACK, W], F32, name="gain")
+        nc.scalar.activation(gain[:], gs_sb[:].unsqueeze(2).to_broadcast([P, PACK, W]), COPY)
+
+        def gather_bytes(picked, plane, jobs):
+            for s, (rows, lst) in enumerate(jobs):
+                nc.vector.tensor_copy(picked[:, cols(s * S, S)], rows[:].indirect(lst[:]))
+            for q in range(4):
+                nc.sync.dma_start(plane[32 * q : 32 * q + 4, :].bitcast(I32), picked[32 * q : 32 * q + 32 : 8, :].bitcast(I32))
+
+        def gather_words(dst, table, lst, first, count):
+            nc.vector.tensor_copy(dst, table[:].indirect(lst[:, entries(first, count)]))
+
+        picked_h = keep.tile([P, 6 * S], U8, name="picked_h", align_bytes=64)
+        gather_bytes(picked_h, plane_h, [(d_rows, l_k1), (d_rows, l_k2), (d_rows, l_k3), (x_rows, l_offs), (x_rows, l_hz), (x_rows, l_hy)])
+
+        sums = [psum.tile([P, S], F32, name="sums%d" % b, tag="sums%d" % b) for b in range(NBLK)]
+        turned = [psum.tile([P, S], F32, name="turned%d" % t, tag="turned%d" % t) for t in range(PACK)]
+        dealt = [keep.tile([P, PACK, P], F32, name="dealt%d" % b, tag="dealt%d" % b) for b in range(NBLK)]
+
+        def mx_pass(acc, x_codes, x_plane, d_codes, d_plane, start, stop):
+            nc.tensor.matmul_mx(
+                out=acc[:], lhsT=x_codes.bitcast(FP8X4), lhsT_scale=x_plane,
+                rhs=d_codes.bitcast(FP8X4), rhs_scale=d_plane, start=start, stop=stop,
+            )
+
+        def deal(dst, acc):
+            nc.scalar.activation(dst[:], acc[:].rearrange("j (m t) -> j t m", t=PACK), COPY, scale=0.0625)
+
+        for s, (l_d, l_x) in enumerate(((l_k1, l_offs), (l_k2, l_hz), (l_k3, l_hy))):
+            dw = keep.tile([P, S], U32, name="dw%d" % s, tag="dw%d" % s, align_bytes=64)
+            xw = keep.tile([P, S], U32, name="xw%d" % s, tag="xw%d" % s, align_bytes=64)
+            gather_words(dw[:], d_table, l_d, 0, S)
+            piece = S if s < 2 else S // 2
+            for first in range(0, S, piece):
+                gather_words(xw[:, cols(first, piece)], x_table, l_x, first, piece)
+                for b in range(first // BLOCK, (first + piece) // BLOCK):
+                    mx_pass(sums[b], xw[:, cols(b * BLOCK, BLOCK)], plane_h[:, cols((3 + s) * S + b * BLOCK, BLOCK)],
+                            dw[:], plane_h[:, cols(s * S, S)], s == 0, s == 2)
+                    if s == 2:
+                        deal(dealt[b], sums[b])
+                        for t in range(PACK):
+                            nc.tensor.transpose(turned[t][:, cols(b * BLOCK, BLOCK)], dealt[b][:, t, :], ident[:])
+
+        picked_h2 = keep.tile([P, 3 * S], U8, name="picked_h2", tag="dw0", align_bytes=64)
+        gather_bytes(picked_h2, plane_h2, [(d_rows, l_k4), (d_rows, l_k5), (x_rows, l_hx)])
+        dw5 = keep.tile([P, S], U32, name="dw5", tag="xw0", align_bytes=64)
+        gather_words(dw5[:], d_table, l_k5, 0, S)
+        hx_head = keep.tile([P, BLOCK], U32, name="hx_head", tag="dw1", align_bytes=64)
+        gather_words(hx_head[:], x_table, l_hx, 0, BLOCK)
+
+        pa, pb = [], []
+        for t in range(PACK):
+            h = keep.tile([P, S], F32, name="h%d" % t)
+            nc.scalar.copy(h[:], turned[t][:])
+            pa.append(keep.tile([P, W], F32, name="pa%d" % t))
+            pb.append(keep.tile([P, W], F32, name="pb%d" % t))
+            nc.scalar.activation(pa[t][:], h[:].indirect(l_n1[:]), COPY)
+            nc.scalar.activation(pb[t][:], h[:].indirect(l_n2[:]), COPY)
+
+        ra = [keep.tile([P, W], F32, name="ra%d" % t, tag="ra%d" % t, align_bytes=64) for t in range(PACK)]
+        rb = [keep.tile([P, W], F32, name="rb%d" % t) for t in range(PACK)]
+        ub = [keep.tile([P, S], F32, name="ub%d" % t) for t in range(PACK)]
+        far = [keep.tile([P, S], F32, name="far%d" % t) for t in range(PACK)]
+        z_rows = keep.tile([P, PACK, S], BF16, name="z_rows", align_bytes=64)
+
+        def sort_pairs(t):
+            nc.vector.tensor_tensor(ra[t][:], pa[t][:], pb[t][:], ALU.max)
+            nc.vector.tensor_tensor(rb[t][:], pa[t][:], pb[t][:], ALU.min)
+
+        def put_larger(t):
+            nc.vector.tensor_tensor(ub[t][:].indirect(l_n1[:]), ra[t][:], gain[:, t, :], ALU.mult)
+
+        def put_smaller(t, piece):
+            nc.vector.tensor_tensor(ub[t][:].indirect(l_n2[:]), rb[t][:], gain[:, t, :], ALU.mult)
+            for first in range(0, S, piece):
+                nc.scalar.activation(far[t][:, cols(first, piece)], ub[t][:].indirect(l_n3[:, entries(first, piece)]), COPY)
+
+        def difference(t, first, count):
+            c = cols(first, count)
+            nc.vector.tensor_tensor(z_rows[:, t, c], ub[t][:, c], far[t][:, c], ALU.subtract)
+
+        sort_pairs(0)
+        for t in range(PACK - 1):
+            put_larger(t)
+            sort_pairs(t + 1)
+            put_smaller(t, W)
+        difference(0, 0, S)
+        put_larger(3)
+        difference(1, 0, S)
+        difference(2, 0, S)
+        put_smaller(3, BLOCK)
+
+        dw4 = keep.tile([P, S], U32, name="dw4", tag="ra3", align_bytes=64)
+        gather_words(dw4[:], d_table, l_k4, 0, S)
+
+        sums2 = [psum.tile([P, S], F32, name="sumsb%d" % b, tag="sums%d" % b) for b in range(NBLK)]
+        turned2 = [psum.tile([P, PACK, BLOCK], F32, name="turnedb%d" % b, tag="turned%d" % b) for b in range(NBLK)]
+        dealt2 = [keep.tile([P, PACK, P], F32, name="dealtb%d" % b, tag="dealt%d" % b) for b in range(NBLK)]
+        z_in = [keep.tile([P, BLOCK * PACK], BF16, name="z_in%d" % b, tag="z_in%d" % b, align_bytes=64) for b in range(NBLK)]
+        z_codes = keep.tile([P, S], U32, name="z_codes", align_bytes=64)
+        z_plane = keep.tile([P, S], U8, name="z_plane", align_bytes=64)
+        h2 = keep.tile([P, PACK, S], F32, name="h2")
+
+        def quantise(b):
+            c = cols(b * BLOCK, BLOCK)
+            nc.scalar.copy(
+                z_in[b][:].rearrange("p (c i t) -> p c t i", i=4, t=PACK),
+                z_rows[:, :, c].rearrange("p t (c i) -> p c t i", i=4),
+            )
+            nc.vector.quantize_mx(out=z_codes[:, c].bitcast(FP8X4), scales=z_plane[:, c], in_=z_in[b][:])
+
+        def second_product(b, hx_codes):
+            c = cols(b * BLOCK, BLOCK)
+            mx_pass(sums2[b], hx_codes, plane_h2[:, cols(2 * S + b * BLOCK, BLOCK)], dw5[:], plane_h2[:, cols(S, S)], True, False)
+            mx_pass(sums2[b], z_codes[:, c], z_plane[:, c], dw4[:], plane_h2[:, cols(0, S)], False, True)
+            deal(dealt2[b], sums2[b])
+            for t in range(PACK):
+                nc.tensor.transpose(turned2[b][:, t, :], dealt2[b][:, t, :], ident[:])
+            nc.scalar.copy(h2[:, :, c], turned2[b][:])
+
+        difference(3, 0, BLOCK)
+        quantise(0)
+        second_product(0, hx_head[:])
+        difference(3, BLOCK, S - BLOCK)
+        hx_rest = keep.tile([P, S - BLOCK], U32, name="hx_rest", tag="z_in0", align_bytes=64)
+        gather_words(hx_rest[:], x_table, l_hx, BLOCK, S - BLOCK)
+        for b in range(1, NBLK):
+            quantise(b)
+            second_product(b, hx_rest[:, cols((b - 1) * BLOCK, BLOCK)])
+
+        ds = [keep.tile([P, S], F32, name="ds%d" % t) for t in range(PACK)]
+        for first, count in ((0, BLOCK), (BLOCK, BLOCK), (2 * BLOCK, 2 * BLOCK)):
+            for t in range(PACK):
+                nc.vector.tensor_copy(ds[t][:].indirect(l_n6[:, entries(first, count)]), h2[:, t, cols(first, count)])
+
+        up = [keep.tile([P, S], F32, name="up%d" % t) for t in range(PACK)]
+        page = [keep.tile([P, U], F32, name="page%d" % t) for t in range(PACK)]
+        out_rows = out.rearrange("(p t) w -> p t w", t=PACK)
+
+        def put_sent(t):
+            nc.vector.tensor_copy(page[t][:].indirect(l_n4[:]), ds[t][:])
+            nc.vector.tensor_tensor(up[t][:], h2[:, t, :], ds[t][:], ALU.max)
+
+        def put_upper(t):
+            nc.vector.tensor_copy(page[t][:].indirect(l_n5[:]), up[t][:])
+            nc.sync.dma_start(out_rows[:, t, :], page[t][:])
+
+        put_sent(0)
+        for t in range(1, PACK):
+            put_sent(t)
+            put_upper(t - 1)
+        put_upper(PACK - 1)

@@ -12,6 +12,7 @@ U8 = mybir.dt.uint8
 FP8X4 = mybir.dt.float8_e4m3fn_x4
 ALU = mybir.AluOpType
 COPY = mybir.ActivationFunctionType.Copy
+RELU = mybir.ActivationFunctionType.Relu
 
 P = 128
 PACK = 4
@@ -51,24 +52,26 @@ def tile_picked_mthhzmhorddpagsn_none_p_kernel(
         x_rows = keep.tile([P, T], U8, name="x_rows", align_bytes=64)
         plane_h = keep.tile([P, 6 * S], U8, name="plane_h", align_bytes=64)
         plane_h2 = keep.tile([P, 3 * S], U8, name="plane_h2", align_bytes=64)
-        for tile in (d_rows, x_rows, plane_h, plane_h2):
+        for tile in (x_rows, d_rows):
+            nc.gpsimd.memset(tile[:].bitcast(I32), 0)
+        for tile in (plane_h, plane_h2):
             nc.vector.memset(tile[:].bitcast(I32), 0)
+        d_table = keep.tile([P, G], U32, name="d_table", align_bytes=64)
+        x_table = keep.tile([P, T], U32, name="x_table", align_bytes=64)
+        l_offs = load_list("l_offs", offs)
+        nc.sync.dma_start(x_table[:].bitcast(I32), x_words[0].rearrange("p n t -> p (n t)").bitcast(I32))
+        l_hz = load_list("l_hz", hz)
+        nc.sync.dma_start(x_rows[0:P:8, :].bitcast(I32), x_scales[0].bitcast(I32))
+        l_hy = load_list("l_hy", hy)
         nc.sync.dma_start(d_rows[0:P:8, :].bitcast(I32), d_scales[0].bitcast(I32))
         l_k1 = load_list("l_k1", k1)
         l_k2 = load_list("l_k2", k2)
         l_k3 = load_list("l_k3", k3)
-        nc.sync.dma_start(x_rows[0:P:8, :].bitcast(I32), x_scales[0].bitcast(I32))
-        l_offs = load_list("l_offs", offs)
-        l_hz = load_list("l_hz", hz)
-        l_hy = load_list("l_hy", hy)
-        d_table = keep.tile([P, G], U32, name="d_table", align_bytes=64)
-        x_table = keep.tile([P, T], U32, name="x_table", align_bytes=64)
-        nc.sync.dma_start(d_table[:].bitcast(I32), d_words[0].rearrange("p n t -> p (n t)").bitcast(I32))
-        nc.sync.dma_start(x_table[:].bitcast(I32), x_words[0].rearrange("p n t -> p (n t)").bitcast(I32))
         gs_sb = keep.tile([P, PACK], F32, name="gs_sb")
         nc.sync.dma_start(gs_sb[:], gs.rearrange("(p t) o -> p (t o)", t=PACK))
         l_k4 = load_list("l_k4", k4)
         l_k5 = load_list("l_k5", k5)
+        nc.sync.dma_start(d_table[:].bitcast(I32), d_words[0].rearrange("p n t -> p (n t)").bitcast(I32))
         l_hx = load_list("l_hx", hx)
         l_n1 = load_list("l_n1", n1)
         l_n2 = load_list("l_n2", n2)
@@ -82,17 +85,26 @@ def tile_picked_mthhzmhorddpagsn_none_p_kernel(
         gain = keep.tile([P, PACK, W], F32, name="gain")
         nc.scalar.activation(gain[:], gs_sb[:].unsqueeze(2).to_broadcast([P, PACK, W]), COPY)
 
-        def gather_bytes(picked, plane, jobs):
+        def gather_bytes(picked, plane, first, jobs):
             for s, (rows, lst) in enumerate(jobs):
                 nc.vector.tensor_copy(picked[:, cols(s * S, S)], rows[:].indirect(lst[:]))
             for q in range(4):
-                nc.sync.dma_start(plane[32 * q : 32 * q + 4, :].bitcast(I32), picked[32 * q : 32 * q + 32 : 8, :].bitcast(I32))
+                nc.sync.dma_start(
+                    plane[32 * q : 32 * q + 4, cols(first, len(jobs) * S)].bitcast(I32),
+                    picked[32 * q : 32 * q + 32 : 8, :].bitcast(I32),
+                )
 
         def gather_words(dst, table, lst, first, count):
             nc.vector.tensor_copy(dst, table[:].indirect(lst[:, entries(first, count)]))
 
-        picked_h = keep.tile([P, 6 * S], U8, name="picked_h", align_bytes=64)
-        gather_bytes(picked_h, plane_h, [(d_rows, l_k1), (d_rows, l_k2), (d_rows, l_k3), (x_rows, l_offs), (x_rows, l_hz), (x_rows, l_hy)])
+        xws = [keep.tile([P, S], U32, name="xw%d" % s, tag="xw%d" % s, align_bytes=64) for s in range(2)]
+        gather_words(xws[0][:], x_table, l_offs, 0, S)
+        gather_words(xws[1][:], x_table, l_hz, 0, S)
+        picked_a = keep.tile([P, 4 * S], U8, name="picked_a", tag="picked_a", align_bytes=64)
+        gather_bytes(picked_a, plane_h, 0, [(x_rows, l_offs), (d_rows, l_k1), (x_rows, l_hz), (d_rows, l_k2)])
+        picked_b = keep.tile([P, 2 * S], U8, name="picked_b", align_bytes=64)
+        gather_bytes(picked_b, plane_h, 4 * S, [(x_rows, l_hy), (d_rows, l_k3)])
+        xws.append(keep.tile([P, S], U32, name="xw2", tag="picked_a", align_bytes=64))
 
         sums = [psum.tile([P, S], F32, name="sums%d" % b, tag="sums%d" % b) for b in range(NBLK)]
         turned = [psum.tile([P, S], F32, name="turned%d" % t, tag="turned%d" % t) for t in range(PACK)]
@@ -107,25 +119,28 @@ def tile_picked_mthhzmhorddpagsn_none_p_kernel(
         def deal(dst, acc):
             nc.scalar.activation(dst[:], acc[:].rearrange("j (m t) -> j t m", t=PACK), COPY, scale=0.0625)
 
-        for s, (l_d, l_x) in enumerate(((l_k1, l_offs), (l_k2, l_hz), (l_k3, l_hy))):
+        for s, l_d in enumerate((l_k1, l_k2, l_k3)):
             dw = keep.tile([P, S], U32, name="dw%d" % s, tag="dw%d" % s, align_bytes=64)
-            xw = keep.tile([P, S], U32, name="xw%d" % s, tag="xw%d" % s, align_bytes=64)
+            xw = xws[s]
             gather_words(dw[:], d_table, l_d, 0, S)
             piece = S if s < 2 else S // 2
             for first in range(0, S, piece):
-                gather_words(xw[:, cols(first, piece)], x_table, l_x, first, piece)
+                if s == 2:
+                    gather_words(xw[:, cols(first, piece)], x_table, l_hy, first, piece)
                 for b in range(first // BLOCK, (first + piece) // BLOCK):
-                    mx_pass(sums[b], xw[:, cols(b * BLOCK, BLOCK)], plane_h[:, cols((3 + s) * S + b * BLOCK, BLOCK)],
-                            dw[:], plane_h[:, cols(s * S, S)], s == 0, s == 2)
+                    mx_pass(sums[b], xw[:, cols(b * BLOCK, BLOCK)], plane_h[:, cols(2 * s * S + b * BLOCK, BLOCK)],
+                            dw[:], plane_h[:, cols((2 * s + 1) * S, S)], s == 0, s == 2)
                     if s == 2:
                         deal(dealt[b], sums[b])
                         for t in range(PACK):
                             nc.tensor.transpose(turned[t][:, cols(b * BLOCK, BLOCK)], dealt[b][:, t, :], ident[:])
 
         picked_h2 = keep.tile([P, 3 * S], U8, name="picked_h2", tag="dw0", align_bytes=64)
-        gather_bytes(picked_h2, plane_h2, [(d_rows, l_k4), (d_rows, l_k5), (x_rows, l_hx)])
+        gather_bytes(picked_h2, plane_h2, 0, [(d_rows, l_k4), (d_rows, l_k5), (x_rows, l_hx)])
         dw5 = keep.tile([P, S], U32, name="dw5", tag="xw0", align_bytes=64)
         gather_words(dw5[:], d_table, l_k5, 0, S)
+        dw4 = keep.tile([P, S], U32, name="dw4", tag="xw1", align_bytes=64)
+        gather_words(dw4[:], d_table, l_k4, 0, S)
         hx_head = keep.tile([P, BLOCK], U32, name="hx_head", tag="dw1", align_bytes=64)
         gather_words(hx_head[:], x_table, l_hx, 0, BLOCK)
 
@@ -139,9 +154,9 @@ def tile_picked_mthhzmhorddpagsn_none_p_kernel(
             nc.scalar.activation(pb[t][:], h[:].indirect(l_n2[:]), COPY)
 
         ra = [keep.tile([P, W], F32, name="ra%d" % t, tag="ra%d" % t, align_bytes=64) for t in range(PACK)]
-        rb = [keep.tile([P, W], F32, name="rb%d" % t) for t in range(PACK)]
+        rb = [keep.tile([P, W], F32, name="rb%d" % t, tag="rb%d" % t, align_bytes=64) for t in range(PACK)]
         ub = [keep.tile([P, S], F32, name="ub%d" % t) for t in range(PACK)]
-        far = [keep.tile([P, S], F32, name="far%d" % t) for t in range(PACK)]
+        far = {}
         z_rows = keep.tile([P, PACK, S], BF16, name="z_rows", align_bytes=64)
 
         def sort_pairs(t):
@@ -151,62 +166,94 @@ def tile_picked_mthhzmhorddpagsn_none_p_kernel(
         def put_larger(t):
             nc.vector.tensor_tensor(ub[t][:].indirect(l_n1[:]), ra[t][:], gain[:, t, :], ALU.mult)
 
-        def put_smaller(t, piece):
+        def put_smaller(t, pieces):
             nc.vector.tensor_tensor(ub[t][:].indirect(l_n2[:]), rb[t][:], gain[:, t, :], ALU.mult)
-            for first in range(0, S, piece):
-                nc.scalar.activation(far[t][:, cols(first, piece)], ub[t][:].indirect(l_n3[:, entries(first, piece)]), COPY)
+            far[t] = keep.tile([P, S], F32, name="far%d" % t, tag="held%d" % (t - 2))
+            for first, count in pieces:
+                nc.scalar.activation(far[t][:, cols(first, count)], ub[t][:].indirect(l_n3[:, entries(first, count)]), COPY, scale=-1.0)
 
         def difference(t, first, count):
             c = cols(first, count)
-            nc.vector.tensor_tensor(z_rows[:, t, c], ub[t][:, c], far[t][:, c], ALU.subtract)
+            nc.vector.tensor_tensor(z_rows[:, t, c], ub[t][:, c], far[t][:, c], ALU.add)
+
+        def add_turned(acc, first, second):
+            nc.tensor.matmul(acc, first, ident[:], is_transpose=True, start=True, stop=False)
+            nc.tensor.matmul(acc, second, ident[:], is_transpose=True, start=False, stop=True)
+
+        def difference_on_tensor(t):
+            across = psum.tile([P, NBLK, P], F32, name="z_across%d" % t, tag="sums%d" % t)
+            back = psum.tile([P, S], F32, name="z_back%d" % t, tag="turned%d" % t)
+            held = keep.tile([P, NBLK, P], F32, name="z_held%d" % t, tag="held%d" % t)
+            for b in range(NBLK):
+                c = cols(b * BLOCK, BLOCK)
+                add_turned(across[:, b, :], ub[t][:, c], far[t][:, c])
+            nc.scalar.copy(held[:], across[:])
+            for b in range(NBLK):
+                nc.tensor.transpose(back[:, cols(b * BLOCK, BLOCK)], held[:, b, :], ident[:])
+            nc.scalar.copy(z_rows[:, t, :], back[:])
 
         sort_pairs(0)
         for t in range(PACK - 1):
             put_larger(t)
             sort_pairs(t + 1)
-            put_smaller(t, W)
-        difference(0, 0, S)
+            put_smaller(t, ((0, W), (W, W)))
+            if t < 2:
+                difference_on_tensor(t)
         put_larger(3)
-        difference(1, 0, S)
+        put_smaller(3, ((0, BLOCK), (BLOCK, BLOCK), (W, W)))
         difference(2, 0, S)
-        put_smaller(3, BLOCK)
 
-        dw4 = keep.tile([P, S], U32, name="dw4", tag="ra3", align_bytes=64)
-        gather_words(dw4[:], d_table, l_k4, 0, S)
 
         sums2 = [psum.tile([P, S], F32, name="sumsb%d" % b, tag="sums%d" % b) for b in range(NBLK)]
-        turned2 = [psum.tile([P, PACK, BLOCK], F32, name="turnedb%d" % b, tag="turned%d" % b) for b in range(NBLK)]
         dealt2 = [keep.tile([P, PACK, P], F32, name="dealtb%d" % b, tag="dealt%d" % b) for b in range(NBLK)]
-        z_in = [keep.tile([P, BLOCK * PACK], BF16, name="z_in%d" % b, tag="z_in%d" % b, align_bytes=64) for b in range(NBLK)]
         z_codes = keep.tile([P, S], U32, name="z_codes", align_bytes=64)
         z_plane = keep.tile([P, S], U8, name="z_plane", align_bytes=64)
         h2 = keep.tile([P, PACK, S], F32, name="h2")
 
-        def quantise(b):
-            c = cols(b * BLOCK, BLOCK)
-            nc.scalar.copy(
-                z_in[b][:].rearrange("p (c i t) -> p c t i", i=4, t=PACK),
+        def interleave(copy, first, count, tag):
+            c = cols(first, count)
+            z_in = keep.tile([P, count * PACK], BF16, name="z_in%d" % first, tag=tag, align_bytes=64)
+            copy(
+                z_in[:].rearrange("p (c i t) -> p c t i", i=4, t=PACK),
                 z_rows[:, :, c].rearrange("p t (c i) -> p c t i", i=4),
             )
-            nc.vector.quantize_mx(out=z_codes[:, c].bitcast(FP8X4), scales=z_plane[:, c], in_=z_in[b][:])
+            return z_in
+
+        def quantise(z_in, first, count):
+            c = cols(first, count)
+            nc.vector.quantize_mx(out=z_codes[:, c].bitcast(FP8X4), scales=z_plane[:, c], in_=z_in[:])
 
         def second_product(b, hx_codes):
             c = cols(b * BLOCK, BLOCK)
             mx_pass(sums2[b], hx_codes, plane_h2[:, cols(2 * S + b * BLOCK, BLOCK)], dw5[:], plane_h2[:, cols(S, S)], True, False)
             mx_pass(sums2[b], z_codes[:, c], z_plane[:, c], dw4[:], plane_h2[:, cols(0, S)], False, True)
-            deal(dealt2[b], sums2[b])
-            for t in range(PACK):
-                nc.tensor.transpose(turned2[b][:, t, :], dealt2[b][:, t, :], ident[:])
-            nc.scalar.copy(h2[:, :, c], turned2[b][:])
+            group = 1 if b == 0 else PACK
+            by_row = sums2[b][:].rearrange("j (m t) -> j t m", t=PACK)
+            waiting = None
+            for t0 in range(0, PACK, group):
+                rows = cols(t0, group)
+                bank = psum.tile([P, group, BLOCK], F32, name="turnedb%d_%d" % (b, t0), tag="turned%d" % (b + t0))
+                nc.scalar.activation(dealt2[b][:, rows, :], by_row[:, rows, :], COPY, scale=0.0625)
+                for t in range(group):
+                    nc.tensor.transpose(bank[:, t, :], dealt2[b][:, t0 + t, :], ident[:])
+                if waiting is not None:
+                    nc.scalar.copy(h2[:, waiting[0], c], waiting[1][:])
+                waiting = (rows, bank)
+            nc.scalar.copy(h2[:, waiting[0], c], waiting[1][:])
 
         difference(3, 0, BLOCK)
-        quantise(0)
+        z_first = interleave(nc.vector.tensor_copy, 0, BLOCK, "z_in0")
+        difference(3, BLOCK, BLOCK)
+        z_second = interleave(nc.scalar.copy, BLOCK, BLOCK, "z_in1")
+        quantise(z_first, 0, BLOCK)
         second_product(0, hx_head[:])
-        difference(3, BLOCK, S - BLOCK)
+        difference(3, W, W)
         hx_rest = keep.tile([P, S - BLOCK], U32, name="hx_rest", tag="z_in0", align_bytes=64)
         gather_words(hx_rest[:], x_table, l_hx, BLOCK, S - BLOCK)
-        for b in range(1, NBLK):
-            quantise(b)
+        quantise(z_second, BLOCK, BLOCK)
+        second_product(1, hx_rest[:, cols(0, BLOCK)])
+        quantise(interleave(nc.vector.tensor_copy, W, W, "z_in1"), W, W)
+        for b in range(2, NBLK):
             second_product(b, hx_rest[:, cols((b - 1) * BLOCK, BLOCK)])
 
         ds = [keep.tile([P, S], F32, name="ds%d" % t) for t in range(PACK)]
@@ -220,12 +267,27 @@ def tile_picked_mthhzmhorddpagsn_none_p_kernel(
 
         def put_sent(t):
             nc.vector.tensor_copy(page[t][:].indirect(l_n4[:]), ds[t][:])
-            nc.vector.tensor_tensor(up[t][:], h2[:, t, :], ds[t][:], ALU.max)
+
+        def upper(t):
+            minus = keep.tile([P, S], F32, name="minus%d" % t)
+            across = psum.tile([P, NBLK, P], F32, name="u_across%d" % t, tag="sums%d" % t)
+            back = psum.tile([P, S], F32, name="u_back%d" % t, tag="turned%d" % t)
+            excess = keep.tile([P, NBLK, P], F32, name="excess%d" % t)
+            nc.scalar.activation(minus[:], h2[:, t, :], COPY, scale=-1.0)
+            for b in range(NBLK):
+                c = cols(b * BLOCK, BLOCK)
+                add_turned(across[:, b, :], ds[t][:, c], minus[:, c])
+            nc.scalar.activation(excess[:], across[:], RELU)
+            for b in range(NBLK):
+                add_turned(back[:, cols(b * BLOCK, BLOCK)], excess[:, b, :], dealt2[b][:, t, :])
+            nc.scalar.copy(up[t][:], back[:])
 
         def put_upper(t):
             nc.vector.tensor_copy(page[t][:].indirect(l_n5[:]), up[t][:])
             nc.sync.dma_start(out_rows[:, t, :], page[t][:])
 
+        for t in range(PACK):
+            upper(t)
         put_sent(0)
         for t in range(1, PACK):
             put_sent(t)

@@ -17,13 +17,19 @@ RELU = mybir.ActivationFunctionType.Relu
 P = 128
 PACK = 4
 S = 512
-W = 256
+HALF = S // 2
 T = 1024
 G = 2048
 U = 1024
 BLOCK = 128
-NBLK = S // BLOCK
-FLOPS = 5 * 2 * 512 * 512 * 512
+BLOCKS = S // BLOCK
+QUADRANT = 32
+ROW_STEP = 8
+GROUP = 16
+RUN = 4
+SIXTEENTH = 0.0625
+DIFFERENCES_ON_TENSOR = 2
+FLOPS = 5 * 2 * S * S * S
 
 
 def cols(first, count):
@@ -31,7 +37,7 @@ def cols(first, count):
 
 
 def entries(first, count):
-    return slice(first // 16, (first + count) // 16)
+    return slice(first // GROUP, (first + count) // GROUP)
 
 
 def tile_picked_mthhzmhorddpagsn_none_p_kernel(
@@ -43,9 +49,9 @@ def tile_picked_mthhzmhorddpagsn_none_p_kernel(
         keep = ctx.enter_context(tc.tile_pool(name="keep", bufs=1))
         psum = ctx.enter_context(tc.psum_pool(name="psum", bufs=1))
 
-        def load_list(name, src):
-            tile = lists.tile([P, src.shape[1]], U16, name=name)
-            nc.sync.dma_start(tile[:], src)
+        def load_list(name, source):
+            tile = lists.tile([P, source.shape[1]], U16, name=name)
+            nc.sync.dma_start(tile[:], source)
             return tile
 
         d_rows = keep.tile([P, G], U8, name="d_rows", align_bytes=64)
@@ -61,14 +67,14 @@ def tile_picked_mthhzmhorddpagsn_none_p_kernel(
         l_offs = load_list("l_offs", offs)
         nc.sync.dma_start(x_table[:].bitcast(I32), x_words[0].rearrange("p n t -> p (n t)").bitcast(I32))
         l_hz = load_list("l_hz", hz)
-        nc.sync.dma_start(x_rows[0:P:8, :].bitcast(I32), x_scales[0].bitcast(I32))
+        nc.sync.dma_start(x_rows[0:P:ROW_STEP, :].bitcast(I32), x_scales[0].bitcast(I32))
         l_hy = load_list("l_hy", hy)
-        nc.sync.dma_start(d_rows[0:P:8, :].bitcast(I32), d_scales[0].bitcast(I32))
+        nc.sync.dma_start(d_rows[0:P:ROW_STEP, :].bitcast(I32), d_scales[0].bitcast(I32))
         l_k1 = load_list("l_k1", k1)
         l_k2 = load_list("l_k2", k2)
         l_k3 = load_list("l_k3", k3)
-        gs_sb = keep.tile([P, PACK], F32, name="gs_sb")
-        nc.sync.dma_start(gs_sb[:], gs.rearrange("(p t) o -> p (t o)", t=PACK))
+        gs_rows = keep.tile([P, PACK], F32, name="gs_rows")
+        nc.sync.dma_start(gs_rows[:], gs.rearrange("(p t) o -> p (t o)", t=PACK))
         l_k4 = load_list("l_k4", k4)
         l_k5 = load_list("l_k5", k5)
         nc.sync.dma_start(d_table[:].bitcast(I32), d_words[0].rearrange("p n t -> p (n t)").bitcast(I32))
@@ -82,61 +88,70 @@ def tile_picked_mthhzmhorddpagsn_none_p_kernel(
 
         ident = keep.tile([P, P], F32, name="ident")
         make_identity(nc, ident[:])
-        gain = keep.tile([P, PACK, W], F32, name="gain")
-        nc.scalar.activation(gain[:], gs_sb[:].unsqueeze(2).to_broadcast([P, PACK, W]), COPY)
+        gain = keep.tile([P, PACK, HALF], F32, name="gain")
+        nc.scalar.activation(gain[:], gs_rows[:].unsqueeze(2).to_broadcast([P, PACK, HALF]), COPY)
 
-        def gather_bytes(picked, plane, first, jobs):
-            for s, (rows, lst) in enumerate(jobs):
-                nc.vector.tensor_copy(picked[:, cols(s * S, S)], rows[:].indirect(lst[:]))
-            for q in range(4):
+        def gather_words(picked, table, offsets, first, count):
+            nc.vector.tensor_copy(picked, table[:].indirect(offsets[:, entries(first, count)]))
+
+        def gather_scales(picked, plane, first, jobs):
+            for s, (rows, offsets) in enumerate(jobs):
+                nc.vector.tensor_copy(picked[:, cols(s * S, S)], rows[:].indirect(offsets[:]))
+            for top in range(0, P, QUADRANT):
                 nc.sync.dma_start(
-                    plane[32 * q : 32 * q + 4, cols(first, len(jobs) * S)].bitcast(I32),
-                    picked[32 * q : 32 * q + 32 : 8, :].bitcast(I32),
+                    plane[top : top + QUADRANT // ROW_STEP, cols(first, len(jobs) * S)].bitcast(I32),
+                    picked[top : top + QUADRANT : ROW_STEP, :].bitcast(I32),
                 )
 
-        def gather_words(dst, table, lst, first, count):
-            nc.vector.tensor_copy(dst, table[:].indirect(lst[:, entries(first, count)]))
-
-        xws = [keep.tile([P, S], U32, name="xw%d" % s, tag="xw%d" % s, align_bytes=64) for s in range(2)]
-        gather_words(xws[0][:], x_table, l_offs, 0, S)
-        gather_words(xws[1][:], x_table, l_hz, 0, S)
-        picked_a = keep.tile([P, 4 * S], U8, name="picked_a", tag="picked_a", align_bytes=64)
-        gather_bytes(picked_a, plane_h, 0, [(x_rows, l_offs), (d_rows, l_k1), (x_rows, l_hz), (d_rows, l_k2)])
-        picked_b = keep.tile([P, 2 * S], U8, name="picked_b", align_bytes=64)
-        gather_bytes(picked_b, plane_h, 4 * S, [(x_rows, l_hy), (d_rows, l_k3)])
-        xws.append(keep.tile([P, S], U32, name="xw2", tag="picked_a", align_bytes=64))
-
-        sums = [psum.tile([P, S], F32, name="sums%d" % b, tag="sums%d" % b) for b in range(NBLK)]
-        turned = [psum.tile([P, S], F32, name="turned%d" % t, tag="turned%d" % t) for t in range(PACK)]
-        dealt = [keep.tile([P, PACK, P], F32, name="dealt%d" % b, tag="dealt%d" % b) for b in range(NBLK)]
-
-        def mx_pass(acc, x_codes, x_plane, d_codes, d_plane, start, stop):
+        def mx_pass(acc, still_codes, still_scales, d_codes, d_plane, start, stop):
             nc.tensor.matmul_mx(
-                out=acc[:], lhsT=x_codes.bitcast(FP8X4), lhsT_scale=x_plane,
+                out=acc[:], lhsT=still_codes.bitcast(FP8X4), lhsT_scale=still_scales,
                 rhs=d_codes.bitcast(FP8X4), rhs_scale=d_plane, start=start, stop=stop,
             )
 
-        def deal(dst, acc):
-            nc.scalar.activation(dst[:], acc[:].rearrange("j (m t) -> j t m", t=PACK), COPY, scale=0.0625)
+        def deal(dealt, acc, tiles):
+            by_tile = acc[:].rearrange("j (m t) -> j t m", t=PACK)
+            nc.scalar.activation(dealt[:, tiles, :], by_tile[:, tiles, :], COPY, scale=SIXTEENTH)
 
-        for s, l_d in enumerate((l_k1, l_k2, l_k3)):
+        def add_turned(acc, first, second):
+            nc.tensor.matmul(acc, first, ident[:], is_transpose=True, start=True, stop=False)
+            nc.tensor.matmul(acc, second, ident[:], is_transpose=True, start=False, stop=True)
+
+        xw = [keep.tile([P, S], U32, name="xw%d" % s, tag="xw%d" % s, align_bytes=64) for s in range(2)]
+        gather_words(xw[0][:], x_table, l_offs, 0, S)
+        gather_words(xw[1][:], x_table, l_hz, 0, S)
+        picked_a = keep.tile([P, 4 * S], U8, name="picked_a", tag="picked_a", align_bytes=64)
+        gather_scales(picked_a, plane_h, 0, [(x_rows, l_offs), (d_rows, l_k1), (x_rows, l_hz), (d_rows, l_k2)])
+        picked_b = keep.tile([P, 2 * S], U8, name="picked_b", align_bytes=64)
+        gather_scales(picked_b, plane_h, 4 * S, [(x_rows, l_hy), (d_rows, l_k3)])
+        xw.append(keep.tile([P, S], U32, name="xw2", tag="picked_a", align_bytes=64))
+
+        h_across = [psum.tile([P, S], F32, name="h_across%d" % b, tag="across%d" % b) for b in range(BLOCKS)]
+        h_rows = [psum.tile([P, S], F32, name="h_rows%d" % t, tag="rows%d" % t) for t in range(PACK)]
+        h_dealt = [keep.tile([P, PACK, P], F32, name="h_dealt%d" % b, tag="dealt%d" % b) for b in range(BLOCKS)]
+
+        def h_pass(s, dw, b):
+            c = cols(b * BLOCK, BLOCK)
+            mx_pass(h_across[b], xw[s][:, c], plane_h[:, cols(2 * s * S + b * BLOCK, BLOCK)],
+                    dw[:], plane_h[:, cols((2 * s + 1) * S, S)], s == 0, s == 2)
+
+        for s, l_d in enumerate((l_k1, l_k2)):
             dw = keep.tile([P, S], U32, name="dw%d" % s, tag="dw%d" % s, align_bytes=64)
-            xw = xws[s]
             gather_words(dw[:], d_table, l_d, 0, S)
-            piece = S if s < 2 else S // 2
-            for first in range(0, S, piece):
-                if s == 2:
-                    gather_words(xw[:, cols(first, piece)], x_table, l_hy, first, piece)
-                for b in range(first // BLOCK, (first + piece) // BLOCK):
-                    mx_pass(sums[b], xw[:, cols(b * BLOCK, BLOCK)], plane_h[:, cols(2 * s * S + b * BLOCK, BLOCK)],
-                            dw[:], plane_h[:, cols((2 * s + 1) * S, S)], s == 0, s == 2)
-                    if s == 2:
-                        deal(dealt[b], sums[b])
-                        for t in range(PACK):
-                            nc.tensor.transpose(turned[t][:, cols(b * BLOCK, BLOCK)], dealt[b][:, t, :], ident[:])
+            for b in range(BLOCKS):
+                h_pass(s, dw, b)
+        dw3 = keep.tile([P, S], U32, name="dw3", align_bytes=64)
+        gather_words(dw3[:], d_table, l_k3, 0, S)
+        for first in range(0, S, HALF):
+            gather_words(xw[2][:, cols(first, HALF)], x_table, l_hy, first, HALF)
+            for b in range(first // BLOCK, (first + HALF) // BLOCK):
+                h_pass(2, dw3, b)
+                deal(h_dealt[b], h_across[b], cols(0, PACK))
+                for t in range(PACK):
+                    nc.tensor.transpose(h_rows[t][:, cols(b * BLOCK, BLOCK)], h_dealt[b][:, t, :], ident[:])
 
         picked_h2 = keep.tile([P, 3 * S], U8, name="picked_h2", tag="dw0", align_bytes=64)
-        gather_bytes(picked_h2, plane_h2, 0, [(d_rows, l_k4), (d_rows, l_k5), (x_rows, l_hx)])
+        gather_scales(picked_h2, plane_h2, 0, [(d_rows, l_k4), (d_rows, l_k5), (x_rows, l_hx)])
         dw5 = keep.tile([P, S], U32, name="dw5", tag="xw0", align_bytes=64)
         gather_words(dw5[:], d_table, l_k5, 0, S)
         dw4 = keep.tile([P, S], U32, name="dw4", tag="xw1", align_bytes=64)
@@ -147,16 +162,16 @@ def tile_picked_mthhzmhorddpagsn_none_p_kernel(
         pa, pb = [], []
         for t in range(PACK):
             h = keep.tile([P, S], F32, name="h%d" % t)
-            nc.scalar.copy(h[:], turned[t][:])
-            pa.append(keep.tile([P, W], F32, name="pa%d" % t))
-            pb.append(keep.tile([P, W], F32, name="pb%d" % t))
+            nc.scalar.copy(h[:], h_rows[t][:])
+            pa.append(keep.tile([P, HALF], F32, name="pa%d" % t))
+            pb.append(keep.tile([P, HALF], F32, name="pb%d" % t))
             nc.scalar.activation(pa[t][:], h[:].indirect(l_n1[:]), COPY)
             nc.scalar.activation(pb[t][:], h[:].indirect(l_n2[:]), COPY)
 
-        ra = [keep.tile([P, W], F32, name="ra%d" % t, tag="ra%d" % t, align_bytes=64) for t in range(PACK)]
-        rb = [keep.tile([P, W], F32, name="rb%d" % t, tag="rb%d" % t, align_bytes=64) for t in range(PACK)]
-        ub = [keep.tile([P, S], F32, name="ub%d" % t) for t in range(PACK)]
-        far = {}
+        ra = [keep.tile([P, HALF], F32, name="ra%d" % t) for t in range(PACK)]
+        rb = [keep.tile([P, HALF], F32, name="rb%d" % t) for t in range(PACK)]
+        weighted = [keep.tile([P, S], F32, name="weighted%d" % t) for t in range(PACK)]
+        far = []
         z_rows = keep.tile([P, PACK, S], BF16, name="z_rows", align_bytes=64)
 
         def sort_pairs(t):
@@ -164,58 +179,62 @@ def tile_picked_mthhzmhorddpagsn_none_p_kernel(
             nc.vector.tensor_tensor(rb[t][:], pa[t][:], pb[t][:], ALU.min)
 
         def put_larger(t):
-            nc.vector.tensor_tensor(ub[t][:].indirect(l_n1[:]), ra[t][:], gain[:, t, :], ALU.mult)
+            nc.vector.tensor_tensor(weighted[t][:].indirect(l_n1[:]), ra[t][:], gain[:, t, :], ALU.mult)
 
-        def put_smaller(t, pieces):
-            nc.vector.tensor_tensor(ub[t][:].indirect(l_n2[:]), rb[t][:], gain[:, t, :], ALU.mult)
-            far[t] = keep.tile([P, S], F32, name="far%d" % t, tag="held%d" % (t - 2))
+        def put_smaller(t):
+            nc.vector.tensor_tensor(weighted[t][:].indirect(l_n2[:]), rb[t][:], gain[:, t, :], ALU.mult)
+
+        def fetch_far(t, tag, pieces):
+            far.append(keep.tile([P, S], F32, name="far%d" % t, tag=tag))
             for first, count in pieces:
-                nc.scalar.activation(far[t][:, cols(first, count)], ub[t][:].indirect(l_n3[:, entries(first, count)]), COPY, scale=-1.0)
+                looked_up = weighted[t][:].indirect(l_n3[:, entries(first, count)])
+                nc.scalar.activation(far[t][:, cols(first, count)], looked_up, COPY, scale=-1.0)
 
-        def difference(t, first, count):
+        def difference_on_vector(t, first, count):
             c = cols(first, count)
-            nc.vector.tensor_tensor(z_rows[:, t, c], ub[t][:, c], far[t][:, c], ALU.add)
-
-        def add_turned(acc, first, second):
-            nc.tensor.matmul(acc, first, ident[:], is_transpose=True, start=True, stop=False)
-            nc.tensor.matmul(acc, second, ident[:], is_transpose=True, start=False, stop=True)
+            nc.vector.tensor_tensor(z_rows[:, t, c], weighted[t][:, c], far[t][:, c], ALU.add)
 
         def difference_on_tensor(t):
-            across = psum.tile([P, NBLK, P], F32, name="z_across%d" % t, tag="sums%d" % t)
-            back = psum.tile([P, S], F32, name="z_back%d" % t, tag="turned%d" % t)
-            held = keep.tile([P, NBLK, P], F32, name="z_held%d" % t, tag="held%d" % t)
-            for b in range(NBLK):
+            across = psum.tile([P, BLOCKS, P], F32, name="z_across%d" % t, tag="across%d" % t)
+            back = psum.tile([P, S], F32, name="z_back%d" % t, tag="rows%d" % t)
+            held = keep.tile([P, BLOCKS, P], F32, name="z_held%d" % t, tag="held%d" % t)
+            for b in range(BLOCKS):
                 c = cols(b * BLOCK, BLOCK)
-                add_turned(across[:, b, :], ub[t][:, c], far[t][:, c])
+                add_turned(across[:, b, :], weighted[t][:, c], far[t][:, c])
             nc.scalar.copy(held[:], across[:])
-            for b in range(NBLK):
+            for b in range(BLOCKS):
                 nc.tensor.transpose(back[:, cols(b * BLOCK, BLOCK)], held[:, b, :], ident[:])
             nc.scalar.copy(z_rows[:, t, :], back[:])
 
+        halves = ((0, HALF), (HALF, HALF))
+        last = PACK - 1
         sort_pairs(0)
-        for t in range(PACK - 1):
+        for t in range(last):
             put_larger(t)
             sort_pairs(t + 1)
-            put_smaller(t, ((0, W), (W, W)))
-            if t < 2:
+            put_smaller(t)
+            if t < DIFFERENCES_ON_TENSOR:
+                fetch_far(t, "far%d" % t, halves)
                 difference_on_tensor(t)
-        put_larger(3)
-        put_smaller(3, ((0, BLOCK), (BLOCK, BLOCK), (W, W)))
-        difference(2, 0, S)
+            else:
+                fetch_far(t, "held%d" % (t - DIFFERENCES_ON_TENSOR), halves)
+        put_larger(last)
+        put_smaller(last)
+        fetch_far(last, "held%d" % (last - DIFFERENCES_ON_TENSOR), ((0, BLOCK), (BLOCK, BLOCK), (HALF, HALF)))
+        for t in range(DIFFERENCES_ON_TENSOR, last):
+            difference_on_vector(t, 0, S)
 
-
-        sums2 = [psum.tile([P, S], F32, name="sumsb%d" % b, tag="sums%d" % b) for b in range(NBLK)]
-        dealt2 = [keep.tile([P, PACK, P], F32, name="dealtb%d" % b, tag="dealt%d" % b) for b in range(NBLK)]
+        h2_across = [psum.tile([P, S], F32, name="h2_across%d" % b, tag="across%d" % b) for b in range(BLOCKS)]
+        h2_dealt = [keep.tile([P, PACK, P], F32, name="h2_dealt%d" % b, tag="dealt%d" % b) for b in range(BLOCKS)]
         z_codes = keep.tile([P, S], U32, name="z_codes", align_bytes=64)
         z_plane = keep.tile([P, S], U8, name="z_plane", align_bytes=64)
         h2 = keep.tile([P, PACK, S], F32, name="h2")
 
         def interleave(copy, first, count, tag):
-            c = cols(first, count)
             z_in = keep.tile([P, count * PACK], BF16, name="z_in%d" % first, tag=tag, align_bytes=64)
             copy(
-                z_in[:].rearrange("p (c i t) -> p c t i", i=4, t=PACK),
-                z_rows[:, :, c].rearrange("p t (c i) -> p c t i", i=4),
+                z_in[:].rearrange("p (c i t) -> p c t i", i=RUN, t=PACK),
+                z_rows[:, :, cols(first, count)].rearrange("p t (c i) -> p c t i", i=RUN),
             )
             return z_in
 
@@ -223,73 +242,70 @@ def tile_picked_mthhzmhorddpagsn_none_p_kernel(
             c = cols(first, count)
             nc.vector.quantize_mx(out=z_codes[:, c].bitcast(FP8X4), scales=z_plane[:, c], in_=z_in[:])
 
-        def second_product(b, hx_codes):
+        def h2_products(b, hx_codes):
             c = cols(b * BLOCK, BLOCK)
-            mx_pass(sums2[b], hx_codes, plane_h2[:, cols(2 * S + b * BLOCK, BLOCK)], dw5[:], plane_h2[:, cols(S, S)], True, False)
-            mx_pass(sums2[b], z_codes[:, c], z_plane[:, c], dw4[:], plane_h2[:, cols(0, S)], False, True)
-            group = 1 if b == 0 else PACK
-            by_row = sums2[b][:].rearrange("j (m t) -> j t m", t=PACK)
-            waiting = None
-            for t0 in range(0, PACK, group):
-                rows = cols(t0, group)
-                bank = psum.tile([P, group, BLOCK], F32, name="turnedb%d_%d" % (b, t0), tag="turned%d" % (b + t0))
-                nc.scalar.activation(dealt2[b][:, rows, :], by_row[:, rows, :], COPY, scale=0.0625)
-                for t in range(group):
-                    nc.tensor.transpose(bank[:, t, :], dealt2[b][:, t0 + t, :], ident[:])
-                if waiting is not None:
-                    nc.scalar.copy(h2[:, waiting[0], c], waiting[1][:])
-                waiting = (rows, bank)
-            nc.scalar.copy(h2[:, waiting[0], c], waiting[1][:])
+            mx_pass(h2_across[b], hx_codes, plane_h2[:, cols(2 * S + b * BLOCK, BLOCK)], dw5[:], plane_h2[:, cols(S, S)], True, False)
+            mx_pass(h2_across[b], z_codes[:, c], z_plane[:, c], dw4[:], plane_h2[:, cols(0, S)], False, True)
 
-        difference(3, 0, BLOCK)
+        def h2_leave(b, first_tile, tiles, bank, copy):
+            rows = cols(first_tile, tiles)
+            turned = psum.tile([P, tiles, BLOCK], F32, name="h2_turned%d_%d" % (b, first_tile), tag="rows%d" % bank)
+            deal(h2_dealt[b], h2_across[b], rows)
+            for t in range(tiles):
+                nc.tensor.transpose(turned[:, t, :], h2_dealt[b][:, first_tile + t, :], ident[:])
+            copy(h2[:, rows, cols(b * BLOCK, BLOCK)], turned[:])
+
+        difference_on_vector(last, 0, BLOCK)
         z_first = interleave(nc.vector.tensor_copy, 0, BLOCK, "z_in0")
-        difference(3, BLOCK, BLOCK)
+        difference_on_vector(last, BLOCK, BLOCK)
         z_second = interleave(nc.scalar.copy, BLOCK, BLOCK, "z_in1")
         quantise(z_first, 0, BLOCK)
-        second_product(0, hx_head[:])
-        difference(3, W, W)
+        h2_products(0, hx_head[:])
+        for t in range(PACK):
+            h2_leave(0, t, 1, t, nc.vector.tensor_copy if t == 0 else nc.scalar.copy)
+        difference_on_vector(last, HALF, HALF)
         hx_rest = keep.tile([P, S - BLOCK], U32, name="hx_rest", tag="z_in0", align_bytes=64)
         gather_words(hx_rest[:], x_table, l_hx, BLOCK, S - BLOCK)
         quantise(z_second, BLOCK, BLOCK)
-        second_product(1, hx_rest[:, cols(0, BLOCK)])
-        quantise(interleave(nc.vector.tensor_copy, W, W, "z_in1"), W, W)
-        for b in range(2, NBLK):
-            second_product(b, hx_rest[:, cols((b - 1) * BLOCK, BLOCK)])
+        h2_products(1, hx_rest[:, cols(0, BLOCK)])
+        h2_leave(1, 0, PACK, 1, nc.scalar.copy)
+        quantise(interleave(nc.vector.tensor_copy, HALF, HALF, "z_in1"), HALF, HALF)
+        for b in range(HALF // BLOCK, BLOCKS):
+            h2_products(b, hx_rest[:, cols((b - 1) * BLOCK, BLOCK)])
+            h2_leave(b, 0, PACK, b, nc.scalar.copy)
 
         ds = [keep.tile([P, S], F32, name="ds%d" % t) for t in range(PACK)]
-        for first, count in ((0, BLOCK), (BLOCK, BLOCK), (2 * BLOCK, 2 * BLOCK)):
+        for first, count in ((0, BLOCK), (BLOCK, BLOCK), (HALF, HALF)):
             for t in range(PACK):
                 nc.vector.tensor_copy(ds[t][:].indirect(l_n6[:, entries(first, count)]), h2[:, t, cols(first, count)])
 
         up = [keep.tile([P, S], F32, name="up%d" % t) for t in range(PACK)]
+        for t in range(PACK):
+            minus_h2 = keep.tile([P, S], F32, name="minus_h2_%d" % t)
+            across = psum.tile([P, BLOCKS, P], F32, name="up_across%d" % t, tag="across%d" % t)
+            back = psum.tile([P, S], F32, name="up_back%d" % t, tag="rows%d" % t)
+            excess = keep.tile([P, BLOCKS, P], F32, name="excess%d" % t)
+            nc.scalar.activation(minus_h2[:], h2[:, t, :], COPY, scale=-1.0)
+            for b in range(BLOCKS):
+                c = cols(b * BLOCK, BLOCK)
+                add_turned(across[:, b, :], ds[t][:, c], minus_h2[:, c])
+            nc.scalar.activation(excess[:], across[:], RELU)
+            for b in range(BLOCKS):
+                add_turned(back[:, cols(b * BLOCK, BLOCK)], excess[:, b, :], h2_dealt[b][:, t, :])
+            nc.scalar.copy(up[t][:], back[:])
+
         page = [keep.tile([P, U], F32, name="page%d" % t) for t in range(PACK)]
         out_rows = out.rearrange("(p t) w -> p t w", t=PACK)
 
         def put_sent(t):
             nc.vector.tensor_copy(page[t][:].indirect(l_n4[:]), ds[t][:])
 
-        def upper(t):
-            minus = keep.tile([P, S], F32, name="minus%d" % t)
-            across = psum.tile([P, NBLK, P], F32, name="u_across%d" % t, tag="sums%d" % t)
-            back = psum.tile([P, S], F32, name="u_back%d" % t, tag="turned%d" % t)
-            excess = keep.tile([P, NBLK, P], F32, name="excess%d" % t)
-            nc.scalar.activation(minus[:], h2[:, t, :], COPY, scale=-1.0)
-            for b in range(NBLK):
-                c = cols(b * BLOCK, BLOCK)
-                add_turned(across[:, b, :], ds[t][:, c], minus[:, c])
-            nc.scalar.activation(excess[:], across[:], RELU)
-            for b in range(NBLK):
-                add_turned(back[:, cols(b * BLOCK, BLOCK)], excess[:, b, :], dealt2[b][:, t, :])
-            nc.scalar.copy(up[t][:], back[:])
-
         def put_upper(t):
             nc.vector.tensor_copy(page[t][:].indirect(l_n5[:]), up[t][:])
             nc.sync.dma_start(out_rows[:, t, :], page[t][:])
 
-        for t in range(PACK):
-            upper(t)
         put_sent(0)
         for t in range(1, PACK):
             put_sent(t)
             put_upper(t - 1)
-        put_upper(PACK - 1)
+        put_upper(last)

from contextlib import ExitStack

import concourse.mybir as mybir
from concourse.masks import make_identity

F32 = mybir.dt.float32
BF16 = mybir.dt.bfloat16
I32 = mybir.dt.int32
U32 = mybir.dt.uint32
U16 = mybir.dt.uint16
U8 = mybir.dt.uint8
FP8X4 = mybir.dt.float8_e4m3fn_x4
ALU = mybir.AluOpType
COPY = mybir.ActivationFunctionType.Copy
RELU = mybir.ActivationFunctionType.Relu

P = 128
PACK = 4
S = 512
HALF = S // 2
T = 1024
G = 2048
U = 1024
BLOCK = 128
BLOCKS = S // BLOCK
QUADRANT = 32
ROW_STEP = 8
GROUP = 16
RUN = 4
SIXTEENTH = 0.0625
DIFFERENCES_ON_TENSOR = 2
FLOPS = 5 * 2 * S * S * S


def cols(first, count):
    return slice(first, first + count)


def entries(first, count):
    return slice(first // GROUP, (first + count) // GROUP)


def tile_picked_mthhzmhorddpagsn_none_p_kernel(
    tc, x_words, x_scales, d_words, d_scales, gs, offs, k1, hz, k2, hy, k3, n1, n2, n3, k4, k5, hx, n4, n5, n6, out
):
    nc = tc.nc
    with ExitStack() as ctx:
        lists = ctx.enter_context(tc.tile_pool(name="lists", bufs=1))
        keep = ctx.enter_context(tc.tile_pool(name="keep", bufs=1))
        psum = ctx.enter_context(tc.psum_pool(name="psum", bufs=1))

        def load_list(name, source):
            tile = lists.tile([P, source.shape[1]], U16, name=name)
            nc.sync.dma_start(tile[:], source)
            return tile

        d_rows = keep.tile([P, G], U8, name="d_rows", align_bytes=64)
        x_rows = keep.tile([P, T], U8, name="x_rows", align_bytes=64)
        plane_h = keep.tile([P, 6 * S], U8, name="plane_h", align_bytes=64)
        plane_h2 = keep.tile([P, 3 * S], U8, name="plane_h2", align_bytes=64)
        for tile in (x_rows, d_rows):
            nc.gpsimd.memset(tile[:].bitcast(I32), 0)
        for tile in (plane_h, plane_h2):
            nc.vector.memset(tile[:].bitcast(I32), 0)
        d_table = keep.tile([P, G], U32, name="d_table", align_bytes=64)
        x_table = keep.tile([P, T], U32, name="x_table", align_bytes=64)
        l_offs = load_list("l_offs", offs)
        nc.sync.dma_start(x_table[:].bitcast(I32), x_words[0].rearrange("p n t -> p (n t)").bitcast(I32))
        l_hz = load_list("l_hz", hz)
        nc.sync.dma_start(x_rows[0:P:ROW_STEP, :].bitcast(I32), x_scales[0].bitcast(I32))
        l_hy = load_list("l_hy", hy)
        nc.sync.dma_start(d_rows[0:P:ROW_STEP, :].bitcast(I32), d_scales[0].bitcast(I32))
        l_k1 = load_list("l_k1", k1)
        l_k2 = load_list("l_k2", k2)
        l_k3 = load_list("l_k3", k3)
        gs_rows = keep.tile([P, PACK], F32, name="gs_rows")
        nc.sync.dma_start(gs_rows[:], gs.rearrange("(p t) o -> p (t o)", t=PACK))
        l_k4 = load_list("l_k4", k4)
        l_k5 = load_list("l_k5", k5)
        nc.sync.dma_start(d_table[:].bitcast(I32), d_words[0].rearrange("p n t -> p (n t)").bitcast(I32))
        l_hx = load_list("l_hx", hx)
        l_n1 = load_list("l_n1", n1)
        l_n2 = load_list("l_n2", n2)
        l_n3 = load_list("l_n3", n3)
        l_n6 = load_list("l_n6", n6)
        l_n4 = load_list("l_n4", n4)
        l_n5 = load_list("l_n5", n5)

        ident = keep.tile([P, P], F32, name="ident")
        make_identity(nc, ident[:])
        gain = keep.tile([P, PACK, HALF], F32, name="gain")
        nc.scalar.activation(gain[:], gs_rows[:].unsqueeze(2).to_broadcast([P, PACK, HALF]), COPY)

        def gather_words(picked, table, offsets, first, count):
            nc.vector.tensor_copy(picked, table[:].indirect(offsets[:, entries(first, count)]))

        def gather_scales(picked, plane, first, jobs):
            for s, (rows, offsets) in enumerate(jobs):
                nc.vector.tensor_copy(picked[:, cols(s * S, S)], rows[:].indirect(offsets[:]))
            for top in range(0, P, QUADRANT):
                nc.sync.dma_start(
                    plane[top : top + QUADRANT // ROW_STEP, cols(first, len(jobs) * S)].bitcast(I32),
                    picked[top : top + QUADRANT : ROW_STEP, :].bitcast(I32),
                )

        def mx_pass(acc, still_codes, still_scales, d_codes, d_plane, start, stop):
            nc.tensor.matmul_mx(
                out=acc[:], lhsT=still_codes.bitcast(FP8X4), lhsT_scale=still_scales,
                rhs=d_codes.bitcast(FP8X4), rhs_scale=d_plane, start=start, stop=stop,
            )

        def deal(dealt, acc, tiles):
            by_tile = acc[:].rearrange("j (m t) -> j t m", t=PACK)
            nc.scalar.activation(dealt[:, tiles, :], by_tile[:, tiles, :], COPY, scale=SIXTEENTH)

        def add_turned(acc, first, second):
            nc.tensor.matmul(acc, first, ident[:], is_transpose=True, start=True, stop=False)
            nc.tensor.matmul(acc, second, ident[:], is_transpose=True, start=False, stop=True)

        xw = [keep.tile([P, S], U32, name="xw%d" % s, tag="xw%d" % s, align_bytes=64) for s in range(2)]
        gather_words(xw[0][:], x_table, l_offs, 0, S)
        gather_words(xw[1][:], x_table, l_hz, 0, S)
        picked_a = keep.tile([P, 4 * S], U8, name="picked_a", tag="picked_a", align_bytes=64)
        gather_scales(picked_a, plane_h, 0, [(x_rows, l_offs), (d_rows, l_k1), (x_rows, l_hz), (d_rows, l_k2)])
        picked_b = keep.tile([P, 2 * S], U8, name="picked_b", align_bytes=64)
        gather_scales(picked_b, plane_h, 4 * S, [(x_rows, l_hy), (d_rows, l_k3)])
        xw.append(keep.tile([P, S], U32, name="xw2", tag="picked_a", align_bytes=64))

        h_across = [psum.tile([P, S], F32, name="h_across%d" % b, tag="across%d" % b) for b in range(BLOCKS)]
        h_rows = [psum.tile([P, S], F32, name="h_rows%d" % t, tag="rows%d" % t) for t in range(PACK)]
        h_dealt = [keep.tile([P, PACK, P], F32, name="h_dealt%d" % b, tag="dealt%d" % b) for b in range(BLOCKS)]

        def h_pass(s, dw, b):
            c = cols(b * BLOCK, BLOCK)
            mx_pass(h_across[b], xw[s][:, c], plane_h[:, cols(2 * s * S + b * BLOCK, BLOCK)],
                    dw[:], plane_h[:, cols((2 * s + 1) * S, S)], s == 0, s == 2)

        for s, l_d in enumerate((l_k1, l_k2)):
            dw = keep.tile([P, S], U32, name="dw%d" % s, tag="dw%d" % s, align_bytes=64)
            gather_words(dw[:], d_table, l_d, 0, S)
            for b in range(BLOCKS):
                h_pass(s, dw, b)
        dw3 = keep.tile([P, S], U32, name="dw3", align_bytes=64)
        gather_words(dw3[:], d_table, l_k3, 0, S)
        for first in range(0, S, HALF):
            gather_words(xw[2][:, cols(first, HALF)], x_table, l_hy, first, HALF)
            for b in range(first // BLOCK, (first + HALF) // BLOCK):
                h_pass(2, dw3, b)
                deal(h_dealt[b], h_across[b], cols(0, PACK))
                for t in range(PACK):
                    nc.tensor.transpose(h_rows[t][:, cols(b * BLOCK, BLOCK)], h_dealt[b][:, t, :], ident[:])

        picked_h2 = keep.tile([P, 3 * S], U8, name="picked_h2", tag="dw0", align_bytes=64)
        gather_scales(picked_h2, plane_h2, 0, [(d_rows, l_k4), (d_rows, l_k5), (x_rows, l_hx)])
        dw5 = keep.tile([P, S], U32, name="dw5", tag="xw0", align_bytes=64)
        gather_words(dw5[:], d_table, l_k5, 0, S)
        dw4 = keep.tile([P, S], U32, name="dw4", tag="xw1", align_bytes=64)
        gather_words(dw4[:], d_table, l_k4, 0, S)
        hx_head = keep.tile([P, BLOCK], U32, name="hx_head", tag="dw1", align_bytes=64)
        gather_words(hx_head[:], x_table, l_hx, 0, BLOCK)

        pa, pb = [], []
        for t in range(PACK):
            h = keep.tile([P, S], F32, name="h%d" % t)
            nc.scalar.copy(h[:], h_rows[t][:])
            pa.append(keep.tile([P, HALF], F32, name="pa%d" % t))
            pb.append(keep.tile([P, HALF], F32, name="pb%d" % t))
            nc.scalar.activation(pa[t][:], h[:].indirect(l_n1[:]), COPY)
            nc.scalar.activation(pb[t][:], h[:].indirect(l_n2[:]), COPY)

        ra = [keep.tile([P, HALF], F32, name="ra%d" % t) for t in range(PACK)]
        rb = [keep.tile([P, HALF], F32, name="rb%d" % t) for t in range(PACK)]
        weighted = [keep.tile([P, S], F32, name="weighted%d" % t) for t in range(PACK)]
        far = []
        z_rows = keep.tile([P, PACK, S], BF16, name="z_rows", align_bytes=64)

        def sort_pairs(t):
            nc.vector.tensor_tensor(ra[t][:], pa[t][:], pb[t][:], ALU.max)
            nc.vector.tensor_tensor(rb[t][:], pa[t][:], pb[t][:], ALU.min)

        def put_larger(t):
            nc.vector.tensor_tensor(weighted[t][:].indirect(l_n1[:]), ra[t][:], gain[:, t, :], ALU.mult)

        def put_smaller(t):
            nc.vector.tensor_tensor(weighted[t][:].indirect(l_n2[:]), rb[t][:], gain[:, t, :], ALU.mult)

        def fetch_far(t, tag, pieces):
            far.append(keep.tile([P, S], F32, name="far%d" % t, tag=tag))
            for first, count in pieces:
                looked_up = weighted[t][:].indirect(l_n3[:, entries(first, count)])
                nc.scalar.activation(far[t][:, cols(first, count)], looked_up, COPY, scale=-1.0)

        def difference_on_vector(t, first, count):
            c = cols(first, count)
            nc.vector.tensor_tensor(z_rows[:, t, c], weighted[t][:, c], far[t][:, c], ALU.add)

        def difference_on_tensor(t):
            across = psum.tile([P, BLOCKS, P], F32, name="z_across%d" % t, tag="across%d" % t)
            back = psum.tile([P, S], F32, name="z_back%d" % t, tag="rows%d" % t)
            held = keep.tile([P, BLOCKS, P], F32, name="z_held%d" % t, tag="held%d" % t)
            for b in range(BLOCKS):
                c = cols(b * BLOCK, BLOCK)
                add_turned(across[:, b, :], weighted[t][:, c], far[t][:, c])
            nc.scalar.copy(held[:], across[:])
            for b in range(BLOCKS):
                nc.tensor.transpose(back[:, cols(b * BLOCK, BLOCK)], held[:, b, :], ident[:])
            nc.scalar.copy(z_rows[:, t, :], back[:])

        halves = ((0, HALF), (HALF, HALF))
        last = PACK - 1
        sort_pairs(0)
        for t in range(last):
            put_larger(t)
            sort_pairs(t + 1)
            put_smaller(t)
            if t < DIFFERENCES_ON_TENSOR:
                fetch_far(t, "far%d" % t, halves)
                difference_on_tensor(t)
            else:
                fetch_far(t, "held%d" % (t - DIFFERENCES_ON_TENSOR), halves)
        put_larger(last)
        put_smaller(last)
        fetch_far(last, "held%d" % (last - DIFFERENCES_ON_TENSOR), ((0, BLOCK), (BLOCK, BLOCK), (HALF, HALF)))
        for t in range(DIFFERENCES_ON_TENSOR, last):
            difference_on_vector(t, 0, S)

        h2_across = [psum.tile([P, S], F32, name="h2_across%d" % b, tag="across%d" % b) for b in range(BLOCKS)]
        h2_dealt = [keep.tile([P, PACK, P], F32, name="h2_dealt%d" % b, tag="dealt%d" % b) for b in range(BLOCKS)]
        z_codes = keep.tile([P, S], U32, name="z_codes", align_bytes=64)
        z_plane = keep.tile([P, S], U8, name="z_plane", align_bytes=64)
        h2 = keep.tile([P, PACK, S], F32, name="h2")

        def interleave(copy, first, count, tag):
            z_in = keep.tile([P, count * PACK], BF16, name="z_in%d" % first, tag=tag, align_bytes=64)
            copy(
                z_in[:].rearrange("p (c i t) -> p c t i", i=RUN, t=PACK),
                z_rows[:, :, cols(first, count)].rearrange("p t (c i) -> p c t i", i=RUN),
            )
            return z_in

        def quantise(z_in, first, count):
            c = cols(first, count)
            nc.vector.quantize_mx(out=z_codes[:, c].bitcast(FP8X4), scales=z_plane[:, c], in_=z_in[:])

        def h2_products(b, hx_codes):
            c = cols(b * BLOCK, BLOCK)
            mx_pass(h2_across[b], hx_codes, plane_h2[:, cols(2 * S + b * BLOCK, BLOCK)], dw5[:], plane_h2[:, cols(S, S)], True, False)
            mx_pass(h2_across[b], z_codes[:, c], z_plane[:, c], dw4[:], plane_h2[:, cols(0, S)], False, True)

        def h2_leave(b, first_tile, tiles, bank, copy):
            rows = cols(first_tile, tiles)
            turned = psum.tile([P, tiles, BLOCK], F32, name="h2_turned%d_%d" % (b, first_tile), tag="rows%d" % bank)
            deal(h2_dealt[b], h2_across[b], rows)
            for t in range(tiles):
                nc.tensor.transpose(turned[:, t, :], h2_dealt[b][:, first_tile + t, :], ident[:])
            copy(h2[:, rows, cols(b * BLOCK, BLOCK)], turned[:])

        difference_on_vector(last, 0, BLOCK)
        z_first = interleave(nc.vector.tensor_copy, 0, BLOCK, "z_in0")
        difference_on_vector(last, BLOCK, BLOCK)
        z_second = interleave(nc.scalar.copy, BLOCK, BLOCK, "z_in1")
        quantise(z_first, 0, BLOCK)
        h2_products(0, hx_head[:])
        for t in range(PACK):
            h2_leave(0, t, 1, t, nc.vector.tensor_copy if t == 0 else nc.scalar.copy)
        difference_on_vector(last, HALF, HALF)
        hx_rest = keep.tile([P, S - BLOCK], U32, name="hx_rest", tag="z_in0", align_bytes=64)
        gather_words(hx_rest[:], x_table, l_hx, BLOCK, S - BLOCK)
        quantise(z_second, BLOCK, BLOCK)
        h2_products(1, hx_rest[:, cols(0, BLOCK)])
        h2_leave(1, 0, PACK, 1, nc.scalar.copy)
        quantise(interleave(nc.vector.tensor_copy, HALF, HALF, "z_in1"), HALF, HALF)
        for b in range(HALF // BLOCK, BLOCKS):
            h2_products(b, hx_rest[:, cols((b - 1) * BLOCK, BLOCK)])
            h2_leave(b, 0, PACK, b, nc.scalar.copy)

        ds = [keep.tile([P, S], F32, name="ds%d" % t) for t in range(PACK)]
        for first, count in ((0, BLOCK), (BLOCK, BLOCK), (HALF, HALF)):
            for t in range(PACK):
                nc.vector.tensor_copy(ds[t][:].indirect(l_n6[:, entries(first, count)]), h2[:, t, cols(first, count)])

        up = [keep.tile([P, S], F32, name="up%d" % t) for t in range(PACK)]
        for t in range(PACK):
            minus_h2 = keep.tile([P, S], F32, name="minus_h2_%d" % t)
            across = psum.tile([P, BLOCKS, P], F32, name="up_across%d" % t, tag="across%d" % t)
            back = psum.tile([P, S], F32, name="up_back%d" % t, tag="rows%d" % t)
            excess = keep.tile([P, BLOCKS, P], F32, name="excess%d" % t)
            nc.scalar.activation(minus_h2[:], h2[:, t, :], COPY, scale=-1.0)
            for b in range(BLOCKS):
                c = cols(b * BLOCK, BLOCK)
                add_turned(across[:, b, :], ds[t][:, c], minus_h2[:, c])
            nc.scalar.activation(excess[:], across[:], RELU)
            for b in range(BLOCKS):
                add_turned(back[:, cols(b * BLOCK, BLOCK)], excess[:, b, :], h2_dealt[b][:, t, :])
            nc.scalar.copy(up[t][:], back[:])

        page = [keep.tile([P, U], F32, name="page%d" % t) for t in range(PACK)]
        out_rows = out.rearrange("(p t) w -> p t w", t=PACK)

        def put_sent(t):
            nc.vector.tensor_copy(page[t][:].indirect(l_n4[:]), ds[t][:])

        def put_upper(t):
            nc.vector.tensor_copy(page[t][:].indirect(l_n5[:]), up[t][:])
            nc.sync.dma_start(out_rows[:, t, :], page[t][:])

        put_sent(0)
        for t in range(1, PACK):
            put_sent(t)
            put_upper(t - 1)
        put_upper(last)
